import numpy as np
import ml_dtypes


def mxq(x, axis, fmt="e4m3"):
    dtype, down = {"e4m3": (ml_dtypes.float8_e4m3fn, 7), "e5m2": (ml_dtypes.float8_e5m2, 14)}[fmt]
    v = np.moveaxis(np.asarray(x, np.float32).astype(ml_dtypes.bfloat16).astype(np.float64), axis, -1)
    blocks = v.reshape(v.shape[:-1] + (-1, 32))
    amax = np.abs(blocks).max(-1, keepdims=True)
    byte = np.maximum(np.where(amax > 0, np.frexp(amax)[1] - 1 + 127, 0) - down, 1)
    scale = np.exp2(byte - 127.0)
    codes = (blocks / scale).astype(np.float32).astype(dtype).astype(np.float64)
    return np.moveaxis((codes * scale).reshape(v.shape), -1, axis)


WIDE = False


def mx_kscale(k):
    if not WIDE:
        return np.ones(k)
    levels = np.array([10, -10, 5, -5, 0])
    if k % 512:
        return np.exp2(np.random.permutation(np.resize(levels, k // 32))).repeat(32)
    a = np.empty((k // 512, 16))
    for p in range(k // 512):
        a[p, :8] = np.random.permutation(np.resize(levels, 8))
        for g in range(8):
            far = levels[np.abs(levels - a[p, g]) >= 10]
            a[p, g + 8] = far[np.random.randint(len(far))]
    return np.exp2(a.ravel()).repeat(32)


def f64(x):
    return np.asarray(x).astype(np.float64)


def striped(idx):
    return np.tile(idx.reshape(-1, 16).T, (8, 1)).astype(np.uint16)


def unstriped(offs):
    return offs[:16].T.reshape(-1).astype(np.int64)


def striped8(idx):
    return np.concatenate([x.reshape(-1, 16).T for x in idx]).astype(np.uint16)


def runs(offs, k):
    lists = np.stack([offs[16 * r : 16 * r + 16].T.reshape(-1) for r in range(8)]).astype(np.int64)
    return lists[np.arange(k) % 512 // 64]


def pack_weight(w):
    k, n = w.shape
    w = f64(np.asarray(w, np.float32).astype(ml_dtypes.bfloat16)).reshape(k // 32, 32, n)
    amax = np.abs(w).max(1)
    byte = np.clip(np.where(amax > 0, np.frexp(amax)[1] - 1 + 127 - 7, 1), 1, 254)
    scaled = (w * np.exp2(127.0 - byte)[:, None, :]).reshape(k, n).astype(np.float32)
    words = np.ascontiguousarray(scaled.reshape(k // 512, 128, 4, n).transpose(0, 1, 3, 2)).astype(ml_dtypes.float8_e4m3fn).view(np.uint8)
    return words, np.ascontiguousarray(byte.astype(np.uint8).reshape(k // 512, 16, n))


def unpack_weight(words, scales):
    g, p, n, _ = words.shape
    vals = np.ascontiguousarray(words).view(ml_dtypes.float8_e4m3fn).astype(np.float64) * np.repeat(np.exp2(scales.astype(np.float64) - 127.0), 8, axis=1)[..., None]
    return vals.transpose(0, 1, 3, 2).reshape(g * 512, n)


def sigmoid(v):
    return 1.0 / (1.0 + np.exp(-np.maximum(v, -700.0)))


K, T, S, H, C = 512, 2048, 512, 512, 512


def setup_inputs():
    n = np.random.standard_normal
    s = mx_kscale(K)[:, None]
    packed_xT = pack_weight(n((K, T)) * s)
    return {
        "x_words": packed_xT[0],
        "x_scales": packed_xT[1],
        "w1": (n((K, H)) / np.sqrt(K) / s).astype(np.float32),
        "gs": (np.random.uniform(0.5, 1.5, (K, 1)) / s).astype(np.float32),
        "offs": striped(np.random.permutation(T)[:S]),
        "n1": striped8(np.stack([np.random.permutation(S) for _ in range(8)])),
        "n2": striped8(np.stack([np.random.permutation(S) for _ in range(8)])),
        "ca": striped(np.random.permutation(T)[:C]),
        "cb": striped(np.random.permutation(T)[:C]),
        "n3": striped8(np.stack([np.random.permutation(S) for _ in range(8)])),
        "n4": striped8(np.stack([np.random.permutation(S) for _ in range(8)])),
        "n5": striped8(np.stack([np.random.permutation(S) for _ in range(8)])),
    }


def reference(x_words, x_scales, w1, gs, offs, n1, n2, ca, cb, n3, n4, n5):
    x_cb = unpack_weight(x_words, x_scales)[:, unstriped(cb)]
    xq = unpack_weight(x_words, x_scales)[:, unstriped(offs)]
    y = mxq(f64(w1), 0, "e4m3").T @ xq
    z = f64(gs) * (y * (sigmoid(y[np.arange(H)[:, None], runs(n1, H)] - (y[np.arange(H)[:, None], runs(n2, H)]))))
    zq = mxq(z, 0, "e4m3")
    b = 0.0625 * (x_cb.T @ zq)
    x_ca = unpack_weight(x_words, x_scales)[:, unstriped(ca)]
    a = 0.0625 * (x_ca.T @ zq)
    return b * (a[np.arange(C)[:, None], runs(n3, C)] - a) + 0.5 * ((b[np.arange(C)[:, None], runs(n5, C)]) * (a[np.arange(C)[:, None], runs(n4, C)] - a))

@@ -1,0 +1,292 @@
+from contextlib import ExitStack
+
+import concourse.mybir as mybir
+
+K, T, S, H, C = 512, 2048, 512, 512, 512
+FLOPS = 2 * K * H * S + 2 * 2 * K * C * S
+
+F32 = mybir.dt.float32
+BF16 = mybir.dt.bfloat16
+I32 = mybir.dt.int32
+U32 = mybir.dt.uint32
+U16 = mybir.dt.uint16
+U8 = mybir.dt.uint8
+FP8X4 = mybir.dt.float8_e4m3fn_x4
+ACT = mybir.ActivationFunctionType
+ALU = mybir.AluOpType
+
+P = 128
+PACK = 4
+HALF = S // 2
+LIST_COLS = S // 16
+HALF_COLS = LIST_COLS // 2
+OPTS = "CAAB"
+CV = (2,)
+UNF = ((3, 1),)
+LAG = 2
+GPS = 0
+
+
+def tile_picked_ccmpflowbcmp_none_p_kernel(
+    tc, x_words, x_scales, w1, gs, offs, n1, n2, ca, cb, n3, n4, n5, out
+):
+    nc = tc.nc
+    with ExitStack() as ctx:
+        keep = ctx.enter_context(tc.tile_pool(name="keep", bufs=1))
+        psum = ctx.enter_context(tc.psum_pool(name="psum", bufs=1))
+
+        def load_list(name, source):
+            offsets = keep.tile([P, LIST_COLS], U16, name=name)
+            nc.sync.dma_start(offsets[:], source)
+            return offsets
+
+        def half_of(offsets, h):
+            return offsets[:, h * HALF_COLS : (h + 1) * HALF_COLS]
+
+        def cols(h):
+            return slice(h * HALF, (h + 1) * HALF)
+
+        table_scales = keep.tile([P, T], U8, align_bytes=64)
+        nc.vector.memset(table_scales[:].bitcast(I32), 0)
+        offs_t = load_list("offs_t", offs)
+        for q in range(4):
+            nc.sync.dma_start(
+                table_scales[32 * q : 32 * q + 4, :].bitcast(I32),
+                x_scales[0, 4 * q : 4 * q + 4, :].bitcast(I32),
+            )
+        w_rows = w1.rearrange("(p j) n -> p j n", j=PACK)
+        w_raw = []
+        for c in range(2):
+            raw = keep.tile([P, PACK, H // 2], F32, name=f"w_raw{c}")
+            nc.sync.dma_start(raw[:], w_rows[:, :, c * (H // 2) : (c + 1) * (H // 2)])
+            w_raw.append(raw)
+        table_words = keep.tile([P, T], U32, align_bytes=64)
+        nc.sync.dma_start(
+            table_words[:].bitcast(I32),
+            x_words[0].rearrange("p n t -> p (n t)").bitcast(I32),
+        )
+        ca_t = load_list("ca_t", ca)
+        cb_t = load_list("cb_t", cb)
+        n2_t = load_list("n2_t", n2)
+        n1_t = load_list("n1_t", n1)
+        gain = keep.tile([P, PACK], F32)
+        nc.sync.dma_start(gain[:], gs.rearrange("(p t) o -> p (t o)", t=PACK))
+        n3_t = load_list("n3_t", n3)
+        n4_t = load_list("n4_t", n4)
+        n5_t = load_list("n5_t", n5)
+
+        w_bf = keep.tile([P, PACK, P, PACK], BF16, align_bytes=64)
+        for c in range(2):
+            nc.scalar.activation(
+                out=w_bf[:, :, c * (P // 2) : (c + 1) * (P // 2), :].rearrange("p t m j -> p m j t"),
+                in_=w_raw[c][:].rearrange("p j (m t) -> p m j t", t=PACK),
+                func=ACT.Copy,
+            )
+
+        xq_words = keep.tile([P, S], U32, align_bytes=64)
+        xq_scales = keep.tile([P, S], U8, align_bytes=64)
+        xa_words = keep.tile([P, PACK, P], U32, align_bytes=64)
+        xa_scales = keep.tile([P, PACK, P], U8, align_bytes=64)
+        xb_words = keep.tile([P, PACK, P], U32, align_bytes=64)
+        xb_scales = keep.tile([P, PACK, P], U8, align_bytes=64)
+        nc.vector.tensor_copy(xq_scales[:], table_scales[:].indirect(offs_t[:]))
+        nc.vector.tensor_copy(xa_scales[:].rearrange("p t m -> p m t"), table_scales[:].indirect(ca_t[:]))
+        nc.vector.tensor_copy(xb_scales[:].rearrange("p t m -> p m t"), table_scales[:].indirect(cb_t[:]))
+
+        w_words = keep.tile([P, H], U32, align_bytes=64)
+        w_scales = keep.tile([P, H], U8, align_bytes=64)
+        nc.vector.quantize_mx(
+            out=w_words[:].bitcast(FP8X4),
+            scales=w_scales[:],
+            in_=w_bf[:].rearrange("p t m j -> p (t m j)"),
+        )
+        nc.vector.tensor_copy(xq_words[:], table_words[:].indirect(offs_t[:]))
+
+        y_bank = []
+        for t in range(PACK):
+            bank = psum.tile([P, S], F32, name=f"y_bank{t}", tag=f"bank{t}")
+            nc.tensor.matmul_mx(
+                out=bank[:],
+                lhsT=w_words[:, t * P : (t + 1) * P].bitcast(FP8X4),
+                lhsT_scale=w_scales[:, t * P : (t + 1) * P],
+                rhs=xq_words[:].bitcast(FP8X4),
+                rhs_scale=xq_scales[:],
+                start=True,
+                stop=True,
+            )
+            y_bank.append(bank)
+
+        nc.vector.tensor_copy(xa_words[:].rearrange("p t m -> p m t"), table_words[:].indirect(ca_t[:]))
+        nc.vector.tensor_copy(xb_words[:].rearrange("p t m -> p m t"), table_words[:].indirect(cb_t[:]))
+
+        y = [keep.tile([P, S], F32, name=f"y{t}") for t in range(PACK)]
+        y_gain = keep.tile([P, PACK, S], F32)
+        sig = [keep.tile([P, PACK, HALF], F32, name=f"sig{h}") for h in range(2)]
+        z_bf = [keep.tile([P, HALF, PACK], BF16, name=f"z_bf{h}", align_bytes=64) for h in range(2)]
+        diff = {}
+        a_bank = [psum.tile([P, S], F32, name=f"a_bank{t}", tag=f"bank{4 + t}") for t in range(PACK)]
+        b_bank = []
+        a = [keep.tile([P, S], F32, name=f"a{t}") for t in range(PACK)]
+        a_twin = {t: keep.tile([P, S], F32, name=f"a_twin{t}") for t in range(PACK) if OPTS[t] == "C"}
+        b_half = [keep.tile([P, S], F32, name=f"b_half{t}") for t in range(PACK)]
+
+        def fetch(dst, window, offsets, h):
+            nc.scalar.activation(out=dst, in_=window[:].indirect(half_of(offsets, h)), func=ACT.Copy)
+
+        def scaled(engine, dst, src, factor):
+            if engine == "S":
+                nc.scalar.activation(out=dst, in_=src, func=ACT.Copy, scale=factor)
+            else:
+                nc.vector.tensor_scalar(dst, src, factor, None, ALU.mult)
+
+        def difference(t, h):
+            if h == 0:
+                if t in CV:
+                    nc.vector.tensor_copy(y[t][:], y_bank[t][:])
+                else:
+                    nc.scalar.copy(y[t][:], y_bank[t][:])
+            second = keep.tile([P, HALF], F32, name=f"second{t}{h}")
+            fetch(second[:], y[t], n2_t, h)
+            d = keep.tile([P, HALF], F32, name=f"diff{t}{h}")
+            if (t, h) in UNF:
+                first = keep.tile([P, HALF], F32, name=f"first{t}{h}")
+                fetch(first[:], y[t], n1_t, h)
+                nc.vector.tensor_tensor(d[:], first[:], second[:], ALU.subtract)
+            else:
+                nc.vector.tensor_tensor(d[:], y[t][:].indirect(half_of(n1_t, h)), second[:], ALU.subtract)
+            diff[(t, h)] = d
+            if h == 0:
+                nc.vector.tensor_scalar(y_gain[:, t, :], y[t][:], gain[:, t : t + 1], None, ALU.mult)
+
+        def gate(t, h):
+            nc.scalar.activation(out=sig[h][:, t, :], in_=diff[(t, h)][:], func=ACT.Sigmoid)
+
+        def make_z(h):
+            nc.vector.tensor_tensor(
+                z_bf[h][:].rearrange("p (c i) t -> p c t i", i=2),
+                y_gain[:, :, cols(h)].rearrange("p t (c i) -> p c t i", i=2),
+                sig[h][:].rearrange("p t (c i) -> p c t i", i=2),
+                ALU.mult,
+            )
+
+        def score(h):
+            z_words = keep.tile([P, HALF], U32, name=f"z_words{h}", align_bytes=64)
+            z_scales = keep.tile([P, HALF], U8, name=f"z_scales{h}", align_bytes=64)
+            nc.vector.quantize_mx(
+                out=z_words[:].bitcast(FP8X4),
+                scales=z_scales[:],
+                in_=z_bf[h][:].rearrange("p n t -> p (n t)"),
+            )
+            if h == 0:
+                for t in range(PACK):
+                    b_bank.append(psum.tile([P, S], F32, name=f"b_bank{t}", tag=f"bank{t}"))
+            for t in range(PACK):
+                for bank, words, scales in ((a_bank[t], xa_words, xa_scales), (b_bank[t], xb_words, xb_scales)):
+                    nc.tensor.matmul_mx(
+                        out=bank[:, cols(h)],
+                        lhsT=words[:, t, :].bitcast(FP8X4),
+                        lhsT_scale=scales[:, t, :],
+                        rhs=z_words[:].bitcast(FP8X4),
+                        rhs_scale=z_scales[:],
+                        start=True,
+                        stop=True,
+                    )
+
+        steps = [(t, h) for h in range(2) for t in range(PACK)]
+        for i, (t, h) in enumerate(steps):
+            difference(t, h)
+            if i >= LAG:
+                gate(*steps[i - LAG])
+            if i == PACK - 1 + LAG:
+                make_z(0)
+            if i == PACK + LAG:
+                score(0)
+        for step in steps[-LAG:]:
+            gate(*step)
+        make_z(1)
+        for t in range(PACK):
+            scaled("S", a[t][:, cols(0)], a_bank[t][:, cols(0)], 0.0625)
+            scaled("S", b_half[t][:, cols(0)], b_bank[t][:, cols(0)], 0.03125)
+            if t in a_twin:
+                scaled("S", a_twin[t][:, cols(0)], a_bank[t][:, cols(0)], 0.0625)
+        score(1)
+
+        out_rows = out.rearrange("(p t) n -> p t n", t=PACK)
+        pending = []
+
+        def finish():
+            if pending:
+                v0, w0, t0 = pending.pop()
+                result = keep.tile([P, S], F32, name=f"result{t0}")
+                adder = nc.gpsimd if t0 < GPS else nc.vector
+                adder.tensor_tensor(result[:], v0[:], w0[:], ALU.add)
+                nc.sync.dma_start(out_rows[:, t0, :], result[:])
+
+        def minus_a(dst, fetched, t, where):
+            nc.vector.scalar_tensor_tensor(
+                out=dst, in0=a_bank[t][:, where], scalar=-0.0625, in1=fetched, op0=ALU.mult, op1=ALU.add
+            )
+
+        def times_b(dst, u, t, where):
+            nc.vector.scalar_tensor_tensor(
+                out=dst, in0=b_bank[t][:, where], scalar=0.0625, in1=u, op0=ALU.mult, op1=ALU.mult
+            )
+
+        whole = slice(0, S)
+        for t in range(PACK):
+            u4 = keep.tile([P, S], F32, name=f"u4_{t}")
+            u3 = keep.tile([P, S], F32, name=f"u3_{t}")
+            a3 = keep.tile([P, S], F32, name=f"a3_{t}")
+            v = keep.tile([P, S], F32, name=f"v{t}")
+            w = keep.tile([P, S], F32, name=f"w{t}")
+            if OPTS[t] == "C":
+                scaled("V" if t == 0 else "S", a[t][:, cols(1)], a_bank[t][:, cols(1)], 0.0625)
+                scaled("S", a_twin[t][:, cols(1)], a_bank[t][:, cols(1)], 0.0625)
+                for h in range(2):
+                    nc.vector.tensor_tensor(
+                        u4[:, cols(h)], a[t][:].indirect(half_of(n4_t, h)), a_twin[t][:, cols(h)], ALU.subtract
+                    )
+                scaled("S", b_half[t][:, cols(1)], b_bank[t][:, cols(1)], 0.03125)
+            else:
+                scaled("S", a[t][:, cols(1)], a_bank[t][:, cols(1)], 0.0625)
+                a4 = keep.tile([P, S], F32, name=f"a4_{t}")
+                for h in range(2):
+                    fetch(a4[:, cols(h)], a[t], n4_t, h)
+                scaled("S", b_half[t][:, cols(1)], b_bank[t][:, cols(1)], 0.03125)
+                minus_a(u4[:], a4[:], t, whole)
+            finish()
+
+            def make_w():
+                if OPTS[t] == "B":
+                    b5 = keep.tile([P, S], F32, name=f"b5_{t}")
+                    for h in range(2):
+                        fetch(b5[:, cols(h)], b_half[t], n5_t, h)
+                    nc.vector.tensor_tensor(w[:], b5[:], u4[:], ALU.mult)
+                else:
+                    for h in range(2):
+                        nc.vector.tensor_tensor(
+                            w[:, cols(h)], b_half[t][:].indirect(half_of(n5_t, h)), u4[:, cols(h)], ALU.mult
+                        )
+
+            late = GPS > 0 and t < PACK - 1
+            if not late:
+                make_w()
+            for h in range(2):
+                fetch(a3[:, cols(h)], a[t], n3_t, h)
+            if t < PACK - 1:
+                minus_a(u3[:], a3[:], t, whole)
+                times_b(v[:], u3[:], t, whole)
+                if late:
+                    make_w()
+                pending.append((v, w, t))
+                if t < GPS:
+                    finish()
+            else:
+                result = keep.tile([P, S], F32, name=f"result{t}")
+                for h in range(2):
+                    minus_a(u3[:, cols(h)], a3[:, cols(h)], t, cols(h))
+                for h in range(2):
+                    times_b(v[:, cols(h)], u3[:, cols(h)], t, cols(h))
+                for h in range(2):
+                    nc.vector.tensor_tensor(result[:, cols(h)], v[:, cols(h)], w[:, cols(h)], ALU.add)
+                    nc.sync.dma_start(out_rows[:, t, cols(h)], result[:, cols(h)])

@@ -75,6 +75,11 @@ def tile_picked_ccmpflowbcmp_none_p_kernel(
         n4_t = load_list("n4_t", n4)
         n5_t = load_list("n5_t", n5)
 
+        warm_in = keep.tile([P, 1], F32)
+        nc.gpsimd.memset(warm_in[:], 0.0)
+        warm_out = keep.tile([P, 1], F32)
+        nc.scalar.activation(out=warm_out[:], in_=warm_in[:], func=ACT.Sigmoid)
+
         w_bf = keep.tile([P, PACK, P, PACK], BF16, align_bytes=64)
         for c in range(2):
             nc.scalar.activation(

@@ -17,6 +17,7 @@ ALU = mybir.AluOpType
 
 P = 128
 PACK = 4
+RUN = 8
 HALF = S // 2
 LIST_COLS = S // 16
 HALF_COLS = LIST_COLS // 2
@@ -47,8 +48,11 @@ def tile_picked_ccmpflowbcmp_none_p_kernel(
             return slice(h * HALF, (h + 1) * HALF)
 
         table_scales = keep.tile([P, T], U8, align_bytes=64)
-        nc.vector.memset(table_scales[:].bitcast(I32), 0)
+        nc.gpsimd.memset(table_scales[:, : T // 2].bitcast(I32), 0)
+        nc.vector.memset(table_scales[:, T // 2 :].bitcast(I32), 0)
         offs_t = load_list("offs_t", offs)
+        ca_t = load_list("ca_t", ca)
+        cb_t = load_list("cb_t", cb)
         for q in range(4):
             nc.sync.dma_start(
                 table_scales[32 * q : 32 * q + 4, :].bitcast(I32),
@@ -65,8 +69,6 @@ def tile_picked_ccmpflowbcmp_none_p_kernel(
             table_words[:].bitcast(I32),
             x_words[0].rearrange("p n t -> p (n t)").bitcast(I32),
         )
-        ca_t = load_list("ca_t", ca)
-        cb_t = load_list("cb_t", cb)
         n2_t = load_list("n2_t", n2)
         n1_t = load_list("n1_t", n1)
         gain = keep.tile([P, PACK], F32)
@@ -95,8 +97,8 @@ def tile_picked_ccmpflowbcmp_none_p_kernel(
         xb_words = keep.tile([P, PACK, P], U32, align_bytes=64)
         xb_scales = keep.tile([P, PACK, P], U8, align_bytes=64)
         nc.vector.tensor_copy(xq_scales[:], table_scales[:].indirect(offs_t[:]))
-        nc.vector.tensor_copy(xa_scales[:].rearrange("p t m -> p m t"), table_scales[:].indirect(ca_t[:]))
-        nc.vector.tensor_copy(xb_scales[:].rearrange("p t m -> p m t"), table_scales[:].indirect(cb_t[:]))
+        nc.vector.tensor_copy(xa_scales[:].rearrange("p t (g i) -> p g t i", i=RUN), table_scales[:].indirect(ca_t[:]))
+        nc.vector.tensor_copy(xb_scales[:].rearrange("p t (g i) -> p g t i", i=RUN), table_scales[:].indirect(cb_t[:]))
 
         w_words = keep.tile([P, H], U32, align_bytes=64)
         w_scales = keep.tile([P, H], U8, align_bytes=64)
@@ -121,8 +123,8 @@ def tile_picked_ccmpflowbcmp_none_p_kernel(
             )
             y_bank.append(bank)
 
-        nc.vector.tensor_copy(xa_words[:].rearrange("p t m -> p m t"), table_words[:].indirect(ca_t[:]))
-        nc.vector.tensor_copy(xb_words[:].rearrange("p t m -> p m t"), table_words[:].indirect(cb_t[:]))
+        nc.vector.tensor_copy(xa_words[:].rearrange("p t (g i) -> p g t i", i=RUN), table_words[:].indirect(ca_t[:]))
+        nc.vector.tensor_copy(xb_words[:].rearrange("p t (g i) -> p g t i", i=RUN), table_words[:].indirect(cb_t[:]))
 
         y = [keep.tile([P, S], F32, name=f"y{t}") for t in range(PACK)]
         y_gain = keep.tile([P, PACK, S], F32)
@@ -131,12 +133,15 @@ def tile_picked_ccmpflowbcmp_none_p_kernel(
         diff = {}
         a_bank = [psum.tile([P, S], F32, name=f"a_bank{t}", tag=f"bank{4 + t}") for t in range(PACK)]
         b_bank = []
-        a = [keep.tile([P, S], F32, name=f"a{t}") for t in range(PACK)]
+        a = [keep.tile([P, 2 * S], F32, name=f"a{t}") for t in range(PACK)]
         a_twin = {t: keep.tile([P, S], F32, name=f"a_twin{t}") for t in range(PACK) if OPTS[t] == "C"}
-        b_half = [keep.tile([P, S], F32, name=f"b_half{t}") for t in range(PACK)]
+        b_half = [keep.tile([P, 2 * S], F32, name=f"b_half{t}") for t in range(PACK)]
 
         def fetch(dst, window, offsets, h):
             nc.scalar.activation(out=dst, in_=window[:].indirect(half_of(offsets, h)), func=ACT.Copy)
+
+        def fetch_all(dst, window, offsets):
+            nc.scalar.activation(out=dst, in_=window[:].indirect(offsets[:]), func=ACT.Copy)
 
         def scaled(engine, dst, src, factor):
             if engine == "S":
@@ -150,21 +155,21 @@ def tile_picked_ccmpflowbcmp_none_p_kernel(
                     nc.vector.tensor_copy(y[t][:], y_bank[t][:])
                 else:
                     nc.scalar.copy(y[t][:], y_bank[t][:])
-            second = keep.tile([P, HALF], F32, name=f"second{t}{h}")
-            fetch(second[:], y[t], n2_t, h)
-            d = keep.tile([P, HALF], F32, name=f"diff{t}{h}")
+            second = a[t][:, S + h * HALF : S + (h + 1) * HALF]
+            fetch(second, y[t], n2_t, h)
+            d = b_half[t][:, S + h * HALF : S + (h + 1) * HALF]
             if (t, h) in UNF:
                 first = keep.tile([P, HALF], F32, name=f"first{t}{h}")
                 fetch(first[:], y[t], n1_t, h)
-                nc.vector.tensor_tensor(d[:], first[:], second[:], ALU.subtract)
+                nc.vector.tensor_tensor(d, first[:], second, ALU.subtract)
             else:
-                nc.vector.tensor_tensor(d[:], y[t][:].indirect(half_of(n1_t, h)), second[:], ALU.subtract)
+                nc.vector.tensor_tensor(d, y[t][:].indirect(half_of(n1_t, h)), second, ALU.subtract)
             diff[(t, h)] = d
             if h == 0:
                 nc.vector.tensor_scalar(y_gain[:, t, :], y[t][:], gain[:, t : t + 1], None, ALU.mult)
 
         def gate(t, h):
-            nc.scalar.activation(out=sig[h][:, t, :], in_=diff[(t, h)][:], func=ACT.Sigmoid)
+            nc.scalar.activation(out=sig[h][:, t, :], in_=diff[(t, h)], func=ACT.Sigmoid)
 
         def make_z(h):
             nc.vector.tensor_tensor(
@@ -216,7 +221,7 @@ def tile_picked_ccmpflowbcmp_none_p_kernel(
                 scaled("S", a_twin[t][:, cols(0)], a_bank[t][:, cols(0)], 0.0625)
         score(1)
 
-        out_rows = out.rearrange("(p t) n -> p t n", t=PACK)
+        out_rows = out.rearrange("(g t i) n -> g i t n", t=PACK, i=RUN)
         pending = []
 
         def finish():
@@ -225,7 +230,7 @@ def tile_picked_ccmpflowbcmp_none_p_kernel(
                 result = keep.tile([P, S], F32, name=f"result{t0}")
                 adder = nc.gpsimd if t0 < GPS else nc.vector
                 adder.tensor_tensor(result[:], v0[:], w0[:], ALU.add)
-                nc.sync.dma_start(out_rows[:, t0, :], result[:])
+                nc.sync.dma_start(out_rows[:, :, t0, :], result[:])
 
         def minus_a(dst, fetched, t, where):
             nc.vector.scalar_tensor_tensor(
@@ -255,8 +260,7 @@ def tile_picked_ccmpflowbcmp_none_p_kernel(
             else:
                 scaled("S", a[t][:, cols(1)], a_bank[t][:, cols(1)], 0.0625)
                 a4 = keep.tile([P, S], F32, name=f"a4_{t}")
-                for h in range(2):
-                    fetch(a4[:, cols(h)], a[t], n4_t, h)
+                fetch_all(a4[:], a[t], n4_t)
                 scaled("S", b_half[t][:, cols(1)], b_bank[t][:, cols(1)], 0.03125)
                 minus_a(u4[:], a4[:], t, whole)
             finish()
@@ -264,21 +268,16 @@ def tile_picked_ccmpflowbcmp_none_p_kernel(
             def make_w():
                 if OPTS[t] == "B":
                     b5 = keep.tile([P, S], F32, name=f"b5_{t}")
-                    for h in range(2):
-                        fetch(b5[:, cols(h)], b_half[t], n5_t, h)
+                    fetch_all(b5[:], b_half[t], n5_t)
                     nc.vector.tensor_tensor(w[:], b5[:], u4[:], ALU.mult)
                 else:
-                    for h in range(2):
-                        nc.vector.tensor_tensor(
-                            w[:, cols(h)], b_half[t][:].indirect(half_of(n5_t, h)), u4[:, cols(h)], ALU.mult
-                        )
+                    nc.vector.tensor_tensor(w[:], b_half[t][:].indirect(n5_t[:]), u4[:], ALU.mult)
 
             late = GPS > 0 and t < PACK - 1
             if not late:
                 make_w()
-            for h in range(2):
-                fetch(a3[:, cols(h)], a[t], n3_t, h)
             if t < PACK - 1:
+                fetch_all(a3[:], a[t], n3_t)
                 minus_a(u3[:], a3[:], t, whole)
                 times_b(v[:], u3[:], t, whole)
                 if late:
@@ -289,9 +288,11 @@ def tile_picked_ccmpflowbcmp_none_p_kernel(
             else:
                 result = keep.tile([P, S], F32, name=f"result{t}")
                 for h in range(2):
+                    fetch(a3[:, cols(h)], a[t], n3_t, h)
+                for h in range(2):
                     minus_a(u3[:, cols(h)], a3[:, cols(h)], t, cols(h))
                 for h in range(2):
                     times_b(v[:, cols(h)], u3[:, cols(h)], t, cols(h))
                 for h in range(2):
                     nc.vector.tensor_tensor(result[:, cols(h)], v[:, cols(h)], w[:, cols(h)], ALU.add)
-                    nc.sync.dma_start(out_rows[:, t, cols(h)], result[:, cols(h)])
+                    nc.sync.dma_start(out_rows[:, :, t, cols(h)], result[:, cols(h)])

@@ -24,8 +24,9 @@ HALF_COLS = LIST_COLS // 2
 OPTS = "CAAB"
 CV = (2,)
 UNF = ((3, 1),)
+UBV = (1,)
 LAG = 2
-GPS = 0
+GPS = 3
 
 
 def tile_picked_ccmpflowbcmp_none_p_kernel(
@@ -85,8 +86,8 @@ def tile_picked_ccmpflowbcmp_none_p_kernel(
         w_bf = keep.tile([P, PACK, P, PACK], BF16, align_bytes=64)
         for c in range(2):
             nc.scalar.activation(
-                out=w_bf[:, :, c * (P // 2) : (c + 1) * (P // 2), :].rearrange("p t m j -> p m j t"),
-                in_=w_raw[c][:].rearrange("p j (m t) -> p m j t", t=PACK),
+                out=w_bf[:, :, c * (P // 2) : (c + 1) * (P // 2), :].rearrange("p t m j -> p m t j"),
+                in_=w_raw[c][:].rearrange("p j (m t) -> p m t j", t=PACK),
                 func=ACT.Copy,
             )
 
@@ -249,50 +250,48 @@ def tile_picked_ccmpflowbcmp_none_p_kernel(
             a3 = keep.tile([P, S], F32, name=f"a3_{t}")
             v = keep.tile([P, S], F32, name=f"v{t}")
             w = keep.tile([P, S], F32, name=f"w{t}")
-            if OPTS[t] == "C":
-                scaled("V" if t == 0 else "S", a[t][:, cols(1)], a_bank[t][:, cols(1)], 0.0625)
+            a4 = keep.tile([P, S], F32, name=f"a4_{t}")
+            if t == 0:
+                scaled("V", a[t][:, cols(1)], a_bank[t][:, cols(1)], 0.0625)
                 scaled("S", a_twin[t][:, cols(1)], a_bank[t][:, cols(1)], 0.0625)
                 for h in range(2):
                     nc.vector.tensor_tensor(
                         u4[:, cols(h)], a[t][:].indirect(half_of(n4_t, h)), a_twin[t][:, cols(h)], ALU.subtract
                     )
+                fetch_all(a3[:], a[t], n3_t)
                 scaled("S", b_half[t][:, cols(1)], b_bank[t][:, cols(1)], 0.03125)
+                minus_a(u3[:], a3[:], t, whole)
+                nc.vector.tensor_tensor(w[:], b_half[t][:].indirect(n5_t[:]), u4[:], ALU.mult)
+                times_b(v[:], u3[:], t, whole)
+            elif t < PACK - 1:
+                scaled("S", a[t][:, cols(1)], a_bank[t][:, cols(1)], 0.0625)
+                fetch_all(a3[:], a[t], n3_t)
+                minus_a(u3[:], a3[:], t, whole)
+                fetch_all(a4[:], a[t], n4_t)
+                minus_a(u4[:], a4[:], t, whole)
+                scaled("V" if t in UBV else "S", b_half[t][:, cols(1)], b_bank[t][:, cols(1)], 0.03125)
+                finish()
+                times_b(v[:], u3[:], t, whole)
+                nc.vector.tensor_tensor(w[:], b_half[t][:].indirect(n5_t[:]), u4[:], ALU.mult)
             else:
                 scaled("S", a[t][:, cols(1)], a_bank[t][:, cols(1)], 0.0625)
-                a4 = keep.tile([P, S], F32, name=f"a4_{t}")
                 fetch_all(a4[:], a[t], n4_t)
                 scaled("S", b_half[t][:, cols(1)], b_bank[t][:, cols(1)], 0.03125)
                 minus_a(u4[:], a4[:], t, whole)
-            finish()
-
-            def make_w():
-                if OPTS[t] == "B":
-                    b5 = keep.tile([P, S], F32, name=f"b5_{t}")
-                    fetch_all(b5[:], b_half[t], n5_t)
-                    nc.vector.tensor_tensor(w[:], b5[:], u4[:], ALU.mult)
-                else:
-                    nc.vector.tensor_tensor(w[:], b_half[t][:].indirect(n5_t[:]), u4[:], ALU.mult)
-
-            late = GPS > 0 and t < PACK - 1
-            if not late:
-                make_w()
-            if t < PACK - 1:
+                finish()
                 fetch_all(a3[:], a[t], n3_t)
                 minus_a(u3[:], a3[:], t, whole)
                 times_b(v[:], u3[:], t, whole)
-                if late:
-                    make_w()
+            if t < PACK - 1:
                 pending.append((v, w, t))
                 if t < GPS:
                     finish()
             else:
                 result = keep.tile([P, S], F32, name=f"result{t}")
+                b5 = keep.tile([P, S], F32, name=f"b5_{t}")
                 for h in range(2):
-                    fetch(a3[:, cols(h)], a[t], n3_t, h)
-                for h in range(2):
-                    minus_a(u3[:, cols(h)], a3[:, cols(h)], t, cols(h))
-                for h in range(2):
-                    times_b(v[:, cols(h)], u3[:, cols(h)], t, cols(h))
+                    fetch(b5[:, cols(h)], b_half[t], n5_t, h)
+                    nc.vector.tensor_tensor(w[:, cols(h)], b5[:, cols(h)], u4[:, cols(h)], ALU.mult)
                 for h in range(2):
                     nc.vector.tensor_tensor(result[:, cols(h)], v[:, cols(h)], w[:, cols(h)], ALU.add)
                     nc.sync.dma_start(out_rows[:, :, t, cols(h)], result[:, cols(h)])

@@ -17,16 +17,14 @@ ALU = mybir.AluOpType
 
 P = 128
 PACK = 4
+LAST = PACK - 1
 RUN = 8
 HALF = S // 2
 LIST_COLS = S // 16
-HALF_COLS = LIST_COLS // 2
-OPTS = "CAAB"
-CV = (2,)
-UNF = ((3, 1),)
-UBV = (1,)
+SCORE_SCALE = 0.0625
 LAG = 2
-GPS = 3
+EARLY_TILES = 2
+B_ON_VECTOR = 1
 
 
 def tile_picked_ccmpflowbcmp_none_p_kernel(
@@ -42,11 +40,25 @@ def tile_picked_ccmpflowbcmp_none_p_kernel(
             nc.sync.dma_start(offsets[:], source)
             return offsets
 
-        def half_of(offsets, h):
-            return offsets[:, h * HALF_COLS : (h + 1) * HALF_COLS]
-
         def cols(h):
             return slice(h * HALF, (h + 1) * HALF)
+
+        def half_of(offsets, h):
+            return offsets[:, h * LIST_COLS // 2 : (h + 1) * LIST_COLS // 2]
+
+        def fetch(dst, window, offsets):
+            nc.scalar.activation(out=dst, in_=window[:].indirect(offsets), func=ACT.Copy)
+
+        def multiply(bank, lhs_words, lhs_scales, rhs_words, rhs_scales):
+            nc.tensor.matmul_mx(
+                out=bank,
+                lhsT=lhs_words.bitcast(FP8X4),
+                lhsT_scale=lhs_scales,
+                rhs=rhs_words.bitcast(FP8X4),
+                rhs_scale=rhs_scales,
+                start=True,
+                stop=True,
+            )
 
         table_scales = keep.tile([P, T], U8, align_bytes=64)
         nc.gpsimd.memset(table_scales[:, : T // 2].bitcast(I32), 0)
@@ -54,16 +66,16 @@ def tile_picked_ccmpflowbcmp_none_p_kernel(
         offs_t = load_list("offs_t", offs)
         ca_t = load_list("ca_t", ca)
         cb_t = load_list("cb_t", cb)
-        for q in range(4):
+        for quadrant in range(4):
             nc.sync.dma_start(
-                table_scales[32 * q : 32 * q + 4, :].bitcast(I32),
-                x_scales[0, 4 * q : 4 * q + 4, :].bitcast(I32),
+                table_scales[32 * quadrant : 32 * quadrant + 4, :].bitcast(I32),
+                x_scales[0, 4 * quadrant : 4 * quadrant + 4, :].bitcast(I32),
             )
         w_rows = w1.rearrange("(p j) n -> p j n", j=PACK)
         w_raw = []
-        for c in range(2):
-            raw = keep.tile([P, PACK, H // 2], F32, name=f"w_raw{c}")
-            nc.sync.dma_start(raw[:], w_rows[:, :, c * (H // 2) : (c + 1) * (H // 2)])
+        for part in range(2):
+            raw = keep.tile([P, PACK, H // 2], F32, name=f"w_raw{part}")
+            nc.sync.dma_start(raw[:], w_rows[:, :, part * (H // 2) : (part + 1) * (H // 2)])
             w_raw.append(raw)
         table_words = keep.tile([P, T], U32, align_bytes=64)
         nc.sync.dma_start(
@@ -84,12 +96,15 @@ def tile_picked_ccmpflowbcmp_none_p_kernel(
         nc.scalar.activation(out=warm_out[:], in_=warm_in[:], func=ACT.Sigmoid)
 
         w_bf = keep.tile([P, PACK, P, PACK], BF16, align_bytes=64)
-        for c in range(2):
+        for part in range(2):
             nc.scalar.activation(
-                out=w_bf[:, :, c * (P // 2) : (c + 1) * (P // 2), :].rearrange("p t m j -> p m t j"),
-                in_=w_raw[c][:].rearrange("p j (m t) -> p m t j", t=PACK),
+                out=w_bf[:, :, part * (P // 2) : (part + 1) * (P // 2), :].rearrange("p t m j -> p m t j"),
+                in_=w_raw[part][:].rearrange("p j (m t) -> p m t j", t=PACK),
                 func=ACT.Copy,
             )
+
+        def dealt(tile):
+            return tile[:].rearrange("p t (g i) -> p g t i", i=RUN)
 
         xq_words = keep.tile([P, S], U32, align_bytes=64)
         xq_scales = keep.tile([P, S], U8, align_bytes=64)
@@ -98,8 +113,8 @@ def tile_picked_ccmpflowbcmp_none_p_kernel(
         xb_words = keep.tile([P, PACK, P], U32, align_bytes=64)
         xb_scales = keep.tile([P, PACK, P], U8, align_bytes=64)
         nc.vector.tensor_copy(xq_scales[:], table_scales[:].indirect(offs_t[:]))
-        nc.vector.tensor_copy(xa_scales[:].rearrange("p t (g i) -> p g t i", i=RUN), table_scales[:].indirect(ca_t[:]))
-        nc.vector.tensor_copy(xb_scales[:].rearrange("p t (g i) -> p g t i", i=RUN), table_scales[:].indirect(cb_t[:]))
+        nc.vector.tensor_copy(dealt(xa_scales), table_scales[:].indirect(ca_t[:]))
+        nc.vector.tensor_copy(dealt(xb_scales), table_scales[:].indirect(cb_t[:]))
 
         w_words = keep.tile([P, H], U32, align_bytes=64)
         w_scales = keep.tile([P, H], U8, align_bytes=64)
@@ -113,70 +128,55 @@ def tile_picked_ccmpflowbcmp_none_p_kernel(
         y_bank = []
         for t in range(PACK):
             bank = psum.tile([P, S], F32, name=f"y_bank{t}", tag=f"bank{t}")
-            nc.tensor.matmul_mx(
-                out=bank[:],
-                lhsT=w_words[:, t * P : (t + 1) * P].bitcast(FP8X4),
-                lhsT_scale=w_scales[:, t * P : (t + 1) * P],
-                rhs=xq_words[:].bitcast(FP8X4),
-                rhs_scale=xq_scales[:],
-                start=True,
-                stop=True,
-            )
+            rows = slice(t * P, (t + 1) * P)
+            multiply(bank[:], w_words[:, rows], w_scales[:, rows], xq_words[:], xq_scales[:])
             y_bank.append(bank)
 
-        nc.vector.tensor_copy(xa_words[:].rearrange("p t (g i) -> p g t i", i=RUN), table_words[:].indirect(ca_t[:]))
-        nc.vector.tensor_copy(xb_words[:].rearrange("p t (g i) -> p g t i", i=RUN), table_words[:].indirect(cb_t[:]))
+        nc.vector.tensor_copy(dealt(xa_words), table_words[:].indirect(ca_t[:]))
+        nc.vector.tensor_copy(dealt(xb_words), table_words[:].indirect(cb_t[:]))
 
         y = [keep.tile([P, S], F32, name=f"y{t}") for t in range(PACK)]
         y_gain = keep.tile([P, PACK, S], F32)
-        sig = [keep.tile([P, PACK, HALF], F32, name=f"sig{h}") for h in range(2)]
+        gate = [keep.tile([P, PACK, HALF], F32, name=f"gate{h}") for h in range(2)]
         z_bf = [keep.tile([P, HALF, PACK], BF16, name=f"z_bf{h}", align_bytes=64) for h in range(2)]
-        diff = {}
-        a_bank = [psum.tile([P, S], F32, name=f"a_bank{t}", tag=f"bank{4 + t}") for t in range(PACK)]
+        a_bank = [psum.tile([P, S], F32, name=f"a_bank{t}", tag=f"bank{PACK + t}") for t in range(PACK)]
         b_bank = []
         a = [keep.tile([P, 2 * S], F32, name=f"a{t}") for t in range(PACK)]
-        a_twin = {t: keep.tile([P, S], F32, name=f"a_twin{t}") for t in range(PACK) if OPTS[t] == "C"}
+        a_twin = keep.tile([P, S], F32)
         b_half = [keep.tile([P, 2 * S], F32, name=f"b_half{t}") for t in range(PACK)]
 
-        def fetch(dst, window, offsets, h):
-            nc.scalar.activation(out=dst, in_=window[:].indirect(half_of(offsets, h)), func=ACT.Copy)
-
-        def fetch_all(dst, window, offsets):
-            nc.scalar.activation(out=dst, in_=window[:].indirect(offsets[:]), func=ACT.Copy)
-
-        def scaled(engine, dst, src, factor):
-            if engine == "S":
-                nc.scalar.activation(out=dst, in_=src, func=ACT.Copy, scale=factor)
-            else:
-                nc.vector.tensor_scalar(dst, src, factor, None, ALU.mult)
+        def upper(window, h):
+            return window[:, S + h * HALF : S + (h + 1) * HALF]
 
         def difference(t, h):
             if h == 0:
-                if t in CV:
-                    nc.vector.tensor_copy(y[t][:], y_bank[t][:])
-                else:
+                if t < EARLY_TILES:
                     nc.scalar.copy(y[t][:], y_bank[t][:])
-            second = a[t][:, S + h * HALF : S + (h + 1) * HALF]
-            fetch(second, y[t], n2_t, h)
-            d = b_half[t][:, S + h * HALF : S + (h + 1) * HALF]
-            if (t, h) in UNF:
-                first = keep.tile([P, HALF], F32, name=f"first{t}{h}")
-                fetch(first[:], y[t], n1_t, h)
-                nc.vector.tensor_tensor(d, first[:], second, ALU.subtract)
+                else:
+                    nc.vector.tensor_copy(y[t][:], y_bank[t][:])
+            fetch(upper(a[t], h), y[t], half_of(n2_t, h))
+            if (t, h) == (LAST, 1):
+                first = keep.tile([P, HALF], F32)
+                fetch(first[:], y[t], half_of(n1_t, h))
+                nc.vector.tensor_tensor(upper(b_half[t], h), first[:], upper(a[t], h), ALU.subtract)
             else:
-                nc.vector.tensor_tensor(d, y[t][:].indirect(half_of(n1_t, h)), second, ALU.subtract)
-            diff[(t, h)] = d
+                nc.vector.tensor_tensor(
+                    upper(b_half[t], h), y[t][:].indirect(half_of(n1_t, h)), upper(a[t], h), ALU.subtract
+                )
             if h == 0:
-                nc.vector.tensor_scalar(y_gain[:, t, :], y[t][:], gain[:, t : t + 1], None, ALU.mult)
+                if t < EARLY_TILES:
+                    nc.gpsimd.tensor_scalar(y_gain[:, t, :], y[t][:], gain[:, t : t + 1], 1.0, ALU.mult, ALU.mult)
+                else:
+                    nc.vector.tensor_scalar(y_gain[:, t, :], y[t][:], gain[:, t : t + 1], None, ALU.mult)
 
-        def gate(t, h):
-            nc.scalar.activation(out=sig[h][:, t, :], in_=diff[(t, h)], func=ACT.Sigmoid)
+        def sigmoid(t, h):
+            nc.scalar.activation(out=gate[h][:, t, :], in_=upper(b_half[t], h), func=ACT.Sigmoid)
 
         def make_z(h):
             nc.vector.tensor_tensor(
                 z_bf[h][:].rearrange("p (c i) t -> p c t i", i=2),
                 y_gain[:, :, cols(h)].rearrange("p t (c i) -> p c t i", i=2),
-                sig[h][:].rearrange("p t (c i) -> p c t i", i=2),
+                gate[h][:].rearrange("p t (c i) -> p c t i", i=2),
                 ALU.mult,
             )
 
@@ -192,105 +192,83 @@ def tile_picked_ccmpflowbcmp_none_p_kernel(
                 for t in range(PACK):
                     b_bank.append(psum.tile([P, S], F32, name=f"b_bank{t}", tag=f"bank{t}"))
             for t in range(PACK):
-                for bank, words, scales in ((a_bank[t], xa_words, xa_scales), (b_bank[t], xb_words, xb_scales)):
-                    nc.tensor.matmul_mx(
-                        out=bank[:, cols(h)],
-                        lhsT=words[:, t, :].bitcast(FP8X4),
-                        lhsT_scale=scales[:, t, :],
-                        rhs=z_words[:].bitcast(FP8X4),
-                        rhs_scale=z_scales[:],
-                        start=True,
-                        stop=True,
-                    )
+                multiply(a_bank[t][:, cols(h)], xa_words[:, t, :], xa_scales[:, t, :], z_words[:], z_scales[:])
+                multiply(b_bank[t][:, cols(h)], xb_words[:, t, :], xb_scales[:, t, :], z_words[:], z_scales[:])
+
+        def unload(dst, bank, h, factor, on_vector=False):
+            if on_vector:
+                nc.vector.tensor_scalar(dst[:, cols(h)], bank[:, cols(h)], factor, None, ALU.mult)
+            else:
+                nc.scalar.activation(out=dst[:, cols(h)], in_=bank[:, cols(h)], func=ACT.Copy, scale=factor)
 
         steps = [(t, h) for h in range(2) for t in range(PACK)]
-        for i, (t, h) in enumerate(steps):
-            difference(t, h)
+        for i, step in enumerate(steps):
+            difference(*step)
             if i >= LAG:
-                gate(*steps[i - LAG])
-            if i == PACK - 1 + LAG:
+                sigmoid(*steps[i - LAG])
+            if i == LAST + LAG:
                 make_z(0)
             if i == PACK + LAG:
                 score(0)
         for step in steps[-LAG:]:
-            gate(*step)
+            sigmoid(*step)
         make_z(1)
         for t in range(PACK):
-            scaled("S", a[t][:, cols(0)], a_bank[t][:, cols(0)], 0.0625)
-            scaled("S", b_half[t][:, cols(0)], b_bank[t][:, cols(0)], 0.03125)
-            if t in a_twin:
-                scaled("S", a_twin[t][:, cols(0)], a_bank[t][:, cols(0)], 0.0625)
+            unload(a[t], a_bank[t], 0, SCORE_SCALE)
+            unload(b_half[t], b_bank[t], 0, SCORE_SCALE / 2)
+            if t == 0:
+                unload(a_twin, a_bank[t], 0, SCORE_SCALE)
         score(1)
 
         out_rows = out.rearrange("(g t i) n -> g i t n", t=PACK, i=RUN)
-        pending = []
 
-        def finish():
-            if pending:
-                v0, w0, t0 = pending.pop()
-                result = keep.tile([P, S], F32, name=f"result{t0}")
-                adder = nc.gpsimd if t0 < GPS else nc.vector
-                adder.tensor_tensor(result[:], v0[:], w0[:], ALU.add)
-                nc.sync.dma_start(out_rows[:, :, t0, :], result[:])
-
-        def minus_a(dst, fetched, t, where):
+        def minus_a(dst, fetched, t):
             nc.vector.scalar_tensor_tensor(
-                out=dst, in0=a_bank[t][:, where], scalar=-0.0625, in1=fetched, op0=ALU.mult, op1=ALU.add
+                out=dst[:], in0=a_bank[t][:], scalar=-SCORE_SCALE, in1=fetched[:], op0=ALU.mult, op1=ALU.add
             )
 
-        def times_b(dst, u, t, where):
+        def times_b(dst, factor, t):
             nc.vector.scalar_tensor_tensor(
-                out=dst, in0=b_bank[t][:, where], scalar=0.0625, in1=u, op0=ALU.mult, op1=ALU.mult
+                out=dst[:], in0=b_bank[t][:], scalar=SCORE_SCALE, in1=factor[:], op0=ALU.mult, op1=ALU.mult
             )
 
-        whole = slice(0, S)
         for t in range(PACK):
             u4 = keep.tile([P, S], F32, name=f"u4_{t}")
             u3 = keep.tile([P, S], F32, name=f"u3_{t}")
             a3 = keep.tile([P, S], F32, name=f"a3_{t}")
             v = keep.tile([P, S], F32, name=f"v{t}")
             w = keep.tile([P, S], F32, name=f"w{t}")
-            a4 = keep.tile([P, S], F32, name=f"a4_{t}")
             if t == 0:
-                scaled("V", a[t][:, cols(1)], a_bank[t][:, cols(1)], 0.0625)
-                scaled("S", a_twin[t][:, cols(1)], a_bank[t][:, cols(1)], 0.0625)
+                unload(a[t], a_bank[t], 1, SCORE_SCALE, on_vector=True)
+                unload(a_twin, a_bank[t], 1, SCORE_SCALE)
                 for h in range(2):
                     nc.vector.tensor_tensor(
-                        u4[:, cols(h)], a[t][:].indirect(half_of(n4_t, h)), a_twin[t][:, cols(h)], ALU.subtract
+                        u4[:, cols(h)], a[t][:].indirect(half_of(n4_t, h)), a_twin[:, cols(h)], ALU.subtract
                     )
-                fetch_all(a3[:], a[t], n3_t)
-                scaled("S", b_half[t][:, cols(1)], b_bank[t][:, cols(1)], 0.03125)
-                minus_a(u3[:], a3[:], t, whole)
+                fetch(a3[:], a[t], n3_t[:])
+                unload(b_half[t], b_bank[t], 1, SCORE_SCALE / 2)
+                minus_a(u3, a3, t)
                 nc.vector.tensor_tensor(w[:], b_half[t][:].indirect(n5_t[:]), u4[:], ALU.mult)
-                times_b(v[:], u3[:], t, whole)
-            elif t < PACK - 1:
-                scaled("S", a[t][:, cols(1)], a_bank[t][:, cols(1)], 0.0625)
-                fetch_all(a3[:], a[t], n3_t)
-                minus_a(u3[:], a3[:], t, whole)
-                fetch_all(a4[:], a[t], n4_t)
-                minus_a(u4[:], a4[:], t, whole)
-                scaled("V" if t in UBV else "S", b_half[t][:, cols(1)], b_bank[t][:, cols(1)], 0.03125)
-                finish()
-                times_b(v[:], u3[:], t, whole)
-                nc.vector.tensor_tensor(w[:], b_half[t][:].indirect(n5_t[:]), u4[:], ALU.mult)
+                times_b(v, u3, t)
             else:
-                scaled("S", a[t][:, cols(1)], a_bank[t][:, cols(1)], 0.0625)
-                fetch_all(a4[:], a[t], n4_t)
-                scaled("S", b_half[t][:, cols(1)], b_bank[t][:, cols(1)], 0.03125)
-                minus_a(u4[:], a4[:], t, whole)
-                finish()
-                fetch_all(a3[:], a[t], n3_t)
-                minus_a(u3[:], a3[:], t, whole)
-                times_b(v[:], u3[:], t, whole)
-            if t < PACK - 1:
-                pending.append((v, w, t))
-                if t < GPS:
-                    finish()
+                a4 = keep.tile([P, S], F32, name=f"a4_{t}")
+                unload(a[t], a_bank[t], 1, SCORE_SCALE)
+                fetch(a3[:], a[t], n3_t[:])
+                minus_a(u3, a3, t)
+                fetch(a4[:], a[t], n4_t[:])
+                minus_a(u4, a4, t)
+                unload(b_half[t], b_bank[t], 1, SCORE_SCALE / 2, on_vector=(t == B_ON_VECTOR))
+                times_b(v, u3, t)
+                if t < LAST:
+                    nc.vector.tensor_tensor(w[:], b_half[t][:].indirect(n5_t[:]), u4[:], ALU.mult)
+            result = keep.tile([P, S], F32, name=f"result{t}")
+            if t < LAST:
+                nc.gpsimd.tensor_tensor(result[:], v[:], w[:], ALU.add)
+                nc.sync.dma_start(out_rows[:, :, t, :], result[:])
             else:
-                result = keep.tile([P, S], F32, name=f"result{t}")
-                b5 = keep.tile([P, S], F32, name=f"b5_{t}")
+                b5 = keep.tile([P, S], F32)
                 for h in range(2):
-                    fetch(b5[:, cols(h)], b_half[t], n5_t, h)
+                    fetch(b5[:, cols(h)], b_half[t], half_of(n5_t, h))
                     nc.vector.tensor_tensor(w[:, cols(h)], b5[:, cols(h)], u4[:, cols(h)], ALU.mult)
                 for h in range(2):
                     nc.vector.tensor_tensor(result[:, cols(h)], v[:, cols(h)], w[:, cols(h)], ALU.add)

from contextlib import ExitStack

import concourse.mybir as mybir

K, T, S, H, C = 512, 2048, 512, 512, 512
FLOPS = 2 * K * H * S + 2 * 2 * K * C * S

F32 = mybir.dt.float32
BF16 = mybir.dt.bfloat16
I32 = mybir.dt.int32
U32 = mybir.dt.uint32
U16 = mybir.dt.uint16
U8 = mybir.dt.uint8
FP8X4 = mybir.dt.float8_e4m3fn_x4
ACT = mybir.ActivationFunctionType
ALU = mybir.AluOpType

P = 128
PACK = 4
LAST = PACK - 1
RUN = 8
HALF = S // 2
LIST_COLS = S // 16
SCORE_SCALE = 0.0625
LAG = 2
EARLY_TILES = 2
B_ON_VECTOR = 1


def tile_picked_ccmpflowbcmp_none_p_kernel(
    tc, x_words, x_scales, w1, gs, offs, n1, n2, ca, cb, n3, n4, n5, out
):
    nc = tc.nc
    with ExitStack() as ctx:
        keep = ctx.enter_context(tc.tile_pool(name="keep", bufs=1))
        psum = ctx.enter_context(tc.psum_pool(name="psum", bufs=1))

        def load_list(name, source):
            offsets = keep.tile([P, LIST_COLS], U16, name=name)
            nc.sync.dma_start(offsets[:], source)
            return offsets

        def cols(h):
            return slice(h * HALF, (h + 1) * HALF)

        def half_of(offsets, h):
            return offsets[:, h * LIST_COLS // 2 : (h + 1) * LIST_COLS // 2]

        def fetch(dst, window, offsets):
            nc.scalar.activation(out=dst, in_=window[:].indirect(offsets), func=ACT.Copy)

        def multiply(bank, lhs_words, lhs_scales, rhs_words, rhs_scales):
            nc.tensor.matmul_mx(
                out=bank,
                lhsT=lhs_words.bitcast(FP8X4),
                lhsT_scale=lhs_scales,
                rhs=rhs_words.bitcast(FP8X4),
                rhs_scale=rhs_scales,
                start=True,
                stop=True,
            )

        table_scales = keep.tile([P, T], U8, align_bytes=64)
        nc.gpsimd.memset(table_scales[:, : T // 2].bitcast(I32), 0)
        nc.vector.memset(table_scales[:, T // 2 :].bitcast(I32), 0)
        offs_t = load_list("offs_t", offs)
        ca_t = load_list("ca_t", ca)
        cb_t = load_list("cb_t", cb)
        for quadrant in range(4):
            nc.sync.dma_start(
                table_scales[32 * quadrant : 32 * quadrant + 4, :].bitcast(I32),
                x_scales[0, 4 * quadrant : 4 * quadrant + 4, :].bitcast(I32),
            )
        w_rows = w1.rearrange("(p j) n -> p j n", j=PACK)
        w_raw = []
        for part in range(2):
            raw = keep.tile([P, PACK, H // 2], F32, name=f"w_raw{part}")
            nc.sync.dma_start(raw[:], w_rows[:, :, part * (H // 2) : (part + 1) * (H // 2)])
            w_raw.append(raw)
        table_words = keep.tile([P, T], U32, align_bytes=64)
        nc.sync.dma_start(
            table_words[:].bitcast(I32),
            x_words[0].rearrange("p n t -> p (n t)").bitcast(I32),
        )
        n2_t = load_list("n2_t", n2)
        n1_t = load_list("n1_t", n1)
        gain = keep.tile([P, PACK], F32)
        nc.sync.dma_start(gain[:], gs.rearrange("(p t) o -> p (t o)", t=PACK))
        n3_t = load_list("n3_t", n3)
        n4_t = load_list("n4_t", n4)
        n5_t = load_list("n5_t", n5)

        warm_in = keep.tile([P, 1], F32)
        nc.gpsimd.memset(warm_in[:], 0.0)
        warm_out = keep.tile([P, 1], F32)
        nc.scalar.activation(out=warm_out[:], in_=warm_in[:], func=ACT.Sigmoid)

        w_bf = keep.tile([P, PACK, P, PACK], BF16, align_bytes=64)
        for part in range(2):
            nc.scalar.activation(
                out=w_bf[:, :, part * (P // 2) : (part + 1) * (P // 2), :].rearrange("p t m j -> p m t j"),
                in_=w_raw[part][:].rearrange("p j (m t) -> p m t j", t=PACK),
                func=ACT.Copy,
            )

        def dealt(tile):
            return tile[:].rearrange("p t (g i) -> p g t i", i=RUN)

        xq_words = keep.tile([P, S], U32, align_bytes=64)
        xq_scales = keep.tile([P, S], U8, align_bytes=64)
        xa_words = keep.tile([P, PACK, P], U32, align_bytes=64)
        xa_scales = keep.tile([P, PACK, P], U8, align_bytes=64)
        xb_words = keep.tile([P, PACK, P], U32, align_bytes=64)
        xb_scales = keep.tile([P, PACK, P], U8, align_bytes=64)
        nc.vector.tensor_copy(xq_scales[:], table_scales[:].indirect(offs_t[:]))
        nc.vector.tensor_copy(dealt(xa_scales), table_scales[:].indirect(ca_t[:]))
        nc.vector.tensor_copy(dealt(xb_scales), table_scales[:].indirect(cb_t[:]))

        w_words = keep.tile([P, H], U32, align_bytes=64)
        w_scales = keep.tile([P, H], U8, align_bytes=64)
        nc.vector.quantize_mx(
            out=w_words[:].bitcast(FP8X4),
            scales=w_scales[:],
            in_=w_bf[:].rearrange("p t m j -> p (t m j)"),
        )
        nc.vector.tensor_copy(xq_words[:], table_words[:].indirect(offs_t[:]))

        y_bank = []
        for t in range(PACK):
            bank = psum.tile([P, S], F32, name=f"y_bank{t}", tag=f"bank{t}")
            rows = slice(t * P, (t + 1) * P)
            multiply(bank[:], w_words[:, rows], w_scales[:, rows], xq_words[:], xq_scales[:])
            y_bank.append(bank)

        nc.vector.tensor_copy(dealt(xa_words), table_words[:].indirect(ca_t[:]))
        nc.vector.tensor_copy(dealt(xb_words), table_words[:].indirect(cb_t[:]))

        y = [keep.tile([P, S], F32, name=f"y{t}") for t in range(PACK)]
        y_gain = keep.tile([P, PACK, S], F32)
        gate = [keep.tile([P, PACK, HALF], F32, name=f"gate{h}") for h in range(2)]
        z_bf = [keep.tile([P, HALF, PACK], BF16, name=f"z_bf{h}", align_bytes=64) for h in range(2)]
        a_bank = [psum.tile([P, S], F32, name=f"a_bank{t}", tag=f"bank{PACK + t}") for t in range(PACK)]
        b_bank = []
        a = [keep.tile([P, 2 * S], F32, name=f"a{t}") for t in range(PACK)]
        a_twin = keep.tile([P, S], F32)
        b_half = [keep.tile([P, 2 * S], F32, name=f"b_half{t}") for t in range(PACK)]

        def upper(window, h):
            return window[:, S + h * HALF : S + (h + 1) * HALF]

        def difference(t, h):
            if h == 0:
                if t < EARLY_TILES:
                    nc.scalar.copy(y[t][:], y_bank[t][:])
                else:
                    nc.vector.tensor_copy(y[t][:], y_bank[t][:])
            fetch(upper(a[t], h), y[t], half_of(n2_t, h))
            if (t, h) == (LAST, 1):
                first = keep.tile([P, HALF], F32)
                fetch(first[:], y[t], half_of(n1_t, h))
                nc.vector.tensor_tensor(upper(b_half[t], h), first[:], upper(a[t], h), ALU.subtract)
            else:
                nc.vector.tensor_tensor(
                    upper(b_half[t], h), y[t][:].indirect(half_of(n1_t, h)), upper(a[t], h), ALU.subtract
                )
            if h == 0:
                if t < EARLY_TILES:
                    nc.gpsimd.tensor_scalar(y_gain[:, t, :], y[t][:], gain[:, t : t + 1], 1.0, ALU.mult, ALU.mult)
                else:
                    nc.vector.tensor_scalar(y_gain[:, t, :], y[t][:], gain[:, t : t + 1], None, ALU.mult)

        def sigmoid(t, h):
            nc.scalar.activation(out=gate[h][:, t, :], in_=upper(b_half[t], h), func=ACT.Sigmoid)

        def make_z(h):
            nc.vector.tensor_tensor(
                z_bf[h][:].rearrange("p (c i) t -> p c t i", i=2),
                y_gain[:, :, cols(h)].rearrange("p t (c i) -> p c t i", i=2),
                gate[h][:].rearrange("p t (c i) -> p c t i", i=2),
                ALU.mult,
            )

        def score(h):
            z_words = keep.tile([P, HALF], U32, name=f"z_words{h}", align_bytes=64)
            z_scales = keep.tile([P, HALF], U8, name=f"z_scales{h}", align_bytes=64)
            nc.vector.quantize_mx(
                out=z_words[:].bitcast(FP8X4),
                scales=z_scales[:],
                in_=z_bf[h][:].rearrange("p n t -> p (n t)"),
            )
            if h == 0:
                for t in range(PACK):
                    b_bank.append(psum.tile([P, S], F32, name=f"b_bank{t}", tag=f"bank{t}"))
            for t in range(PACK):
                multiply(a_bank[t][:, cols(h)], xa_words[:, t, :], xa_scales[:, t, :], z_words[:], z_scales[:])
                multiply(b_bank[t][:, cols(h)], xb_words[:, t, :], xb_scales[:, t, :], z_words[:], z_scales[:])

        def unload(dst, bank, h, factor, on_vector=False):
            if on_vector:
                nc.vector.tensor_scalar(dst[:, cols(h)], bank[:, cols(h)], factor, None, ALU.mult)
            else:
                nc.scalar.activation(out=dst[:, cols(h)], in_=bank[:, cols(h)], func=ACT.Copy, scale=factor)

        steps = [(t, h) for h in range(2) for t in range(PACK)]
        for i, step in enumerate(steps):
            difference(*step)
            if i >= LAG:
                sigmoid(*steps[i - LAG])
            if i == LAST + LAG:
                make_z(0)
            if i == PACK + LAG:
                score(0)
        for step in steps[-LAG:]:
            sigmoid(*step)
        make_z(1)
        for t in range(PACK):
            unload(a[t], a_bank[t], 0, SCORE_SCALE)
            unload(b_half[t], b_bank[t], 0, SCORE_SCALE / 2)
            if t == 0:
                unload(a_twin, a_bank[t], 0, SCORE_SCALE)
        score(1)

        out_rows = out.rearrange("(g t i) n -> g i t n", t=PACK, i=RUN)

        def minus_a(dst, fetched, t):
            nc.vector.scalar_tensor_tensor(
                out=dst[:], in0=a_bank[t][:], scalar=-SCORE_SCALE, in1=fetched[:], op0=ALU.mult, op1=ALU.add
            )

        def times_b(dst, factor, t):
            nc.vector.scalar_tensor_tensor(
                out=dst[:], in0=b_bank[t][:], scalar=SCORE_SCALE, in1=factor[:], op0=ALU.mult, op1=ALU.mult
            )

        for t in range(PACK):
            u4 = keep.tile([P, S], F32, name=f"u4_{t}")
            u3 = keep.tile([P, S], F32, name=f"u3_{t}")
            a3 = keep.tile([P, S], F32, name=f"a3_{t}")
            v = keep.tile([P, S], F32, name=f"v{t}")
            w = keep.tile([P, S], F32, name=f"w{t}")
            if t == 0:
                unload(a[t], a_bank[t], 1, SCORE_SCALE, on_vector=True)
                unload(a_twin, a_bank[t], 1, SCORE_SCALE)
                for h in range(2):
                    nc.vector.tensor_tensor(
                        u4[:, cols(h)], a[t][:].indirect(half_of(n4_t, h)), a_twin[:, cols(h)], ALU.subtract
                    )
                fetch(a3[:], a[t], n3_t[:])
                unload(b_half[t], b_bank[t], 1, SCORE_SCALE / 2)
                minus_a(u3, a3, t)
                nc.vector.tensor_tensor(w[:], b_half[t][:].indirect(n5_t[:]), u4[:], ALU.mult)
                times_b(v, u3, t)
            else:
                a4 = keep.tile([P, S], F32, name=f"a4_{t}")
                unload(a[t], a_bank[t], 1, SCORE_SCALE)
                fetch(a3[:], a[t], n3_t[:])
                minus_a(u3, a3, t)
                fetch(a4[:], a[t], n4_t[:])
                minus_a(u4, a4, t)
                unload(b_half[t], b_bank[t], 1, SCORE_SCALE / 2, on_vector=(t == B_ON_VECTOR))
                times_b(v, u3, t)
                if t < LAST:
                    nc.vector.tensor_tensor(w[:], b_half[t][:].indirect(n5_t[:]), u4[:], ALU.mult)
            result = keep.tile([P, S], F32, name=f"result{t}")
            if t < LAST:
                nc.gpsimd.tensor_tensor(result[:], v[:], w[:], ALU.add)
                nc.sync.dma_start(out_rows[:, :, t, :], result[:])
            else:
                b5 = keep.tile([P, S], F32)
                for h in range(2):
                    fetch(b5[:, cols(h)], b_half[t], half_of(n5_t, h))
                    nc.vector.tensor_tensor(w[:, cols(h)], b5[:, cols(h)], u4[:, cols(h)], ALU.mult)
                for h in range(2):
                    nc.vector.tensor_tensor(result[:, cols(h)], v[:, cols(h)], w[:, cols(h)], ALU.add)
                    nc.sync.dma_start(out_rows[:, :, t, cols(h)], result[:, cols(h)])
